import numpy as np
import ml_dtypes


def mxq(x, axis, fmt="e4m3"):
    dtype, down = {"e4m3": (ml_dtypes.float8_e4m3fn, 7), "e5m2": (ml_dtypes.float8_e5m2, 14)}[fmt]
    v = np.moveaxis(np.asarray(x, np.float32).astype(ml_dtypes.bfloat16).astype(np.float64), axis, -1)
    blocks = v.reshape(v.shape[:-1] + (-1, 32))
    amax = np.abs(blocks).max(-1, keepdims=True)
    byte = np.maximum(np.where(amax > 0, np.frexp(amax)[1] - 1 + 127, 0) - down, 1)
    scale = np.exp2(byte - 127.0)
    codes = (blocks / scale).astype(np.float32).astype(dtype).astype(np.float64)
    return np.moveaxis((codes * scale).reshape(v.shape), -1, axis)


WIDE = False


def mx_kscale(k):
    if not WIDE:
        return np.ones(k)
    levels = np.array([10, -10, 5, -5, 0])
    if k % 512:
        return np.exp2(np.random.permutation(np.resize(levels, k // 32))).repeat(32)
    a = np.empty((k // 512, 16))
    for p in range(k // 512):
        a[p, :8] = np.random.permutation(np.resize(levels, 8))
        for g in range(8):
            far = levels[np.abs(levels - a[p, g]) >= 10]
            a[p, g + 8] = far[np.random.randint(len(far))]
    return np.exp2(a.ravel()).repeat(32)


def f64(x):
    return np.asarray(x).astype(np.float64)


def striped(idx):
    return np.tile(idx.reshape(-1, 16).T, (8, 1)).astype(np.uint16)


def unstriped(offs):
    return offs[:16].T.reshape(-1).astype(np.int64)


E2M1 = np.array([0.0, 0.5, 1.0, 1.5, 2.0, 3.0, 4.0, 6.0, -0.0, -0.5, -1.0, -1.5, -2.0, -3.0, -4.0, -6.0])


def pack_weight(w, fmt):
    k, n = w.shape
    w = f64(np.asarray(w, np.float32).astype(ml_dtypes.bfloat16)).reshape(k // 32, 32, n)
    amax = np.abs(w).max(1)
    if fmt == "e4m3":
        byte = np.frexp(amax)[1] - 1 + 127 - 7
    else:
        mant, ex = np.frexp(amax / 6.0)
        byte = np.where(mant > 0.5, ex, ex - 1) + 127
    byte = np.clip(np.where(amax > 0, byte, 1), 1, 254)
    scaled = (w * np.exp2(127.0 - byte)[:, None, :]).reshape(k, n).astype(np.float32)
    by_word = np.ascontiguousarray(scaled.reshape(k // 512, 128, 4, n).transpose(0, 1, 3, 2))
    if fmt == "e4m3":
        words = by_word.astype(ml_dtypes.float8_e4m3fn).view(np.uint8)
    else:
        c = by_word.astype(ml_dtypes.float4_e2m1fn).view(np.uint8) & 0xF
        words = (c[..., 0::2] | (c[..., 1::2] << 4)).reshape(k // 512, 128, 2 * n)
    return np.ascontiguousarray(words), np.ascontiguousarray(byte.astype(np.uint8).reshape(k // 512, 16, n))


def unpack_weight(words, scales, fmt):
    g, _, n = scales.shape
    words = np.ascontiguousarray(words).reshape(g, 128, n, -1)
    if fmt == "e4m3":
        vals = words.view(ml_dtypes.float8_e4m3fn).astype(np.float64)
    else:
        nib = np.empty((g, 128, n, 4), np.uint8)
        nib[..., 0::2] = words & 0xF
        nib[..., 1::2] = words >> 4
        vals = E2M1[nib]
    vals = vals * np.repeat(np.exp2(scales.astype(np.float64) - 127.0), 8, axis=1)[..., None]
    return vals.transpose(0, 1, 3, 2).reshape(g * 512, n)


def gelu(v):
    return 0.5 * v * (1.0 + np.tanh(np.sqrt(2.0 / np.pi) * (v + 0.044715 * v**3)))


def bf(x):
    return np.asarray(x, np.float32).astype(ml_dtypes.bfloat16)


def planes(Y):
    n, m = Y.shape
    b = f64(bf(Y)).reshape(n // 32, 32, m)
    amax = np.abs(b).max(1)
    byte = np.clip(np.where(amax > 0, np.frexp(amax)[1] - 1 + 127 - 7, 1), 1, 254)
    codes = (b * np.exp2(127.0 - byte)[:, None, :]).reshape(n, m).astype(np.float32).astype(ml_dtypes.float8_e4m3fn).view(np.uint8)
    words = codes.reshape(n // 512, 128, 4, m).transpose(0, 1, 3, 2)
    return np.ascontiguousarray(words), np.ascontiguousarray(byte.astype(np.uint8).reshape(n // 512, 16, m))


K, H, N, T, S, T2, P = 1536, 1024, 384, 2048, 512, 1024, 512

def setup_inputs():
    n = np.random.standard_normal
    s = mx_kscale(K)[:, None]
    u = mx_kscale(H)[:, None]
    d = {}
    d["tab_words"], d["tab_scales"] = pack_weight(n((K, T)) * s, "e4m3")
    d["offs"] = striped(np.random.permutation(T)[:S])
    d["offs2"] = striped(np.random.permutation(T2)[:S])
    d["offs3"] = striped(np.random.permutation(T2)[:P])
    d["w1"] = (1.4 * n((K, H)) / K**0.5 / s).astype(np.float32)
    d["gain"] = (1.2 * np.exp(0.3 * n(H)) * u[:, 0]).astype(np.float32)
    d["wgs"] = np.exp(0.3 * n((128, S))).astype(np.float32)
    d["page0"] = (n((H, T2)) * u).astype(np.float32)
    d["bx"] = (0.6 * n(H) * u[:, 0]).astype(np.float32)
    d["w2"] = (n((H, N)) / H**0.5 / u).astype(np.float32)
    d["w3_words"], d["w3_scales"] = pack_weight(n((H, N)) / H**0.5 / u, "e2m1")
    d["w4_words"], d["w4_scales"] = pack_weight(n((H, N)) / H**0.5 / u, "e4m3")
    return d

def reference(tab_words, tab_scales, offs, offs2, offs3, w1, gain, wgs, page0, bx, w2, w3_words, w3_scales, w4_words, w4_scales):
    v = unpack_weight(tab_words, tab_scales, "e4m3")[:, unstriped(offs)]
    e = mxq(f64(w1), 0, "e4m3").T @ v
    h = f64(gain)[:, None] * np.tanh(e)
    page = f64(page0).copy()
    page[:, unstriped(offs2)] = np.tile(f64(wgs), (H // 128, 1)) * h
    x = page[:, unstriped(offs3)] + f64(bx)[:, None]
    xq = mxq(x, 0, "e4m3")
    y2 = mxq(f64(w2), 0, "e4m3").T @ xq
    y3 = unpack_weight(w3_words, w3_scales, "e2m1").T @ xq
    y4 = unpack_weight(w4_words, w4_scales, "e4m3").T @ xq
    y = y2 * y3 + y4
    words, scales = planes(page)
    return y, page, words, scales

@@ -1,0 +1,310 @@
+from contextlib import ExitStack
+
+import concourse.mybir as mybir
+from concourse.masks import make_identity
+
+K, H, N, T, S, T2, M = 1536, 1024, 384, 2048, 512, 1024, 512
+FLOPS = 2 * K * H * S + 3 * 2 * H * N * M
+
+F32 = mybir.dt.float32
+BF16 = mybir.dt.bfloat16
+I32 = mybir.dt.int32
+U32 = mybir.dt.uint32
+U16 = mybir.dt.uint16
+U8 = mybir.dt.uint8
+FP8X4 = mybir.dt.float8_e4m3fn_x4
+FP4X4 = mybir.dt.float4_e2m1fn_x4
+ACT = mybir.ActivationFunctionType
+ALU = mybir.AluOpType
+
+P = 128
+PACK = 4
+PASS = P * PACK
+K_PASSES = K // PASS
+H_PASSES = H // PASS
+N_TILES = N // P
+QUADS = 4
+CHUNK = PACK * PASS
+
+
+def tile_list_hint_slot_features_kernel(
+    tc, tab_words, tab_scales, offs, offs2, offs3, w1, gain, wgs, page0, bx, w2,
+    w3_words, w3_scales, w4_words, w4_scales, out_0, out_1, out_2, out_3,
+):
+    nc = tc.nc
+    with ExitStack() as ctx:
+        sb = ctx.enter_context(tc.tile_pool(name="sb", bufs=1))
+        ps = ctx.enter_context(tc.psum_pool(name="ps", bufs=1))
+
+        def tile(name, shape, dtype, tag=None):
+            return sb.tile(shape, dtype, name=name, tag=tag or name, align_bytes=64)
+
+        banks = [ps.tile([P, 512], F32, name=f"bank{i}") for i in range(8)]
+
+        list1 = tile("list1", [P, S // 16], U16)
+        list2 = tile("list2", [P, S // 16], U16)
+        list3 = tile("list3", [P, M // 16], U16)
+        tab_w = [tile(f"tab_w{a}", [P, T], I32) for a in range(K_PASSES)]
+        tab_rows = tile("tab_rows", [P, T // 4], I32)
+        tab_s = tile("tab_s", [P, T], U8)
+        v_w = [tile(f"v_w{a}", [P, S], U32) for a in range(K_PASSES - 1)]
+        v_s = tile("v_s", [P, S], U8)
+        work = tile("work", [P, H_PASSES * K_PASSES * CHUNK], F32)
+        page = [[tile(f"page{b}{t}", [P, T2], F32) for t in range(PACK)] for b in range(H_PASSES)]
+        wgs_rows = tile("wgs_rows", [P, S], F32)
+        wgs_turned = tile("wgs_turned", [P, S // P * PACK * P], F32)
+        factor = [[tile(f"factor{b}{t}", [P, S], F32) for t in range(PACK)] for b in range(H_PASSES)]
+        tanh_e = [tile(f"tanh_e{t}", [P, S], F32) for t in range(PACK)]
+        gain_c = tile("gain_c", [P, H_PASSES, PACK], F32)
+        bx_c = tile("bx_c", [P, H_PASSES, PACK], F32)
+        w2_raw = [tile(f"w2_raw{b}", [P, PACK, N], F32) for b in range(H_PASSES)]
+        w2_w = tile("w2_w", [P, H_PASSES * N], U32)
+        w2_s = tile("w2_s", [P, H_PASSES * N], U8)
+        w3_w = tile("w3_w", [P, H_PASSES, 2 * N], U8)
+        w3_s = tile("w3_s", [P, H_PASSES, N], U8)
+        w4_w = tile("w4_w", [P, H_PASSES, N], I32)
+        w4_s = tile("w4_s", [P, H_PASSES, N], U8)
+        ident = tile("ident", [P, P], F32)
+        zero = tile("zero", [P, 8], F32)
+        zero_bias = tile("zero_bias", [P, 8], F32)
+        stage = [tile(f"stage{i}", [P, CHUNK], BF16) for i in range(2)]
+        w1_w = [[tile(f"w1_w{b}{a}", [P, PASS], U32) for a in range(K_PASSES)] for b in range(H_PASSES)]
+        w1_s = [[tile(f"w1_s{b}{a}", [P, PASS], U8) for a in range(K_PASSES)] for b in range(H_PASSES)]
+        x_w = [tile(f"x_w{b}", [P, M], U32) for b in range(H_PASSES)]
+        x_s = [tile(f"x_s{b}", [P, M], U8) for b in range(H_PASSES)]
+        page_bf = tile("page_bf", [P, T2 * PACK], BF16)
+        plane_w = [tile(f"plane_w{b}", [P, T2], U32) for b in range(H_PASSES)]
+        plane_s = tile("plane_s", [P, H_PASSES, T2], U8)
+
+        def chunk(i, count=1):
+            return work[:, i * CHUNK : (i + count) * CHUNK]
+
+        w1_raw = [[chunk(b * K_PASSES + a) for a in range(K_PASSES)] for b in range(H_PASSES)]
+        joined = [work[:, 3 * T2 : 7 * T2], work[:, 0 : 4 * T2]]
+        w2_bf = chunk(4).bitcast(BF16)
+        picked = [chunk(5), work[:, 5 * T2 : 7 * T2]]
+
+        w1_rows = w1.rearrange("(a p j) (b c) -> b a p j c", p=P, j=PACK, b=H_PASSES)
+        page_in = page0.rearrange("(b p t) m -> b t p m", p=P, t=PACK)
+        page_out = out_1.rearrange("(b p t) m -> b t p m", p=P, t=PACK)
+        w2_rows = w2.rearrange("(b p j) n -> b p j n", p=P, j=PACK)
+
+        def load_w1(b, a):
+            nc.sync.dma_start(out=w1_raw[b][a].rearrange("p (j c) -> p j c", j=PACK), in_=w1_rows[b, a])
+
+        def load_page(b, t):
+            nc.sync.dma_start(out=page[b][t][:], in_=page_in[b, t])
+
+        nc.sync.dma_start(out=wgs_rows[:], in_=wgs)
+        load_w1(0, 0)
+        load_w1(0, 1)
+        live = [slice(32 * q, 32 * q + 4 * K_PASSES) for q in range(QUADS)]
+        for q in range(QUADS):
+            nc.sync.dma_start(out=tab_rows[live[q], :], in_=tab_scales[:, 4 * q : 4 * q + 4, :].bitcast(I32))
+        nc.sync.dma_start(out=gain_c[:], in_=gain.rearrange("(b p t) -> p b t", p=P, t=PACK))
+        nc.sync.dma_start(list1[:], offs)
+        load_w1(0, 2)
+        for a in range(K_PASSES):
+            nc.sync.dma_start(out=tab_w[a][:], in_=tab_words[a].rearrange("p t i -> p (t i)").bitcast(I32))
+        nc.sync.dma_start(list2[:], offs2)
+        load_page(0, 0)
+        for a in range(K_PASSES):
+            load_page(0, a + 1)
+            load_w1(1, a)
+        for b in range(H_PASSES):
+            nc.sync.dma_start(out=w2_raw[b][:], in_=w2_rows[b])
+        nc.sync.dma_start(list3[:], offs3)
+        nc.sync.dma_start(out=bx_c[:], in_=bx.rearrange("(b p t) -> p b t", p=P, t=PACK))
+        for plane in (w3_s, w4_s):
+            nc.gpsimd.memset(plane[:].bitcast(I32), 0)
+        for q in range(QUADS):
+            load_page(1, q)
+            for plane, rows in ((w3_s, w3_scales), (w4_s, w4_scales)):
+                nc.sync.dma_start(
+                    out=plane[32 * q : 32 * q + 4, :, :].bitcast(I32),
+                    in_=rows[:, 4 * q : 4 * q + 4, :].rearrange("b r n -> r b n").bitcast(I32),
+                )
+        nc.sync.dma_start(out=w3_w[:].bitcast(I32), in_=w3_words.rearrange("b p c -> p b c").bitcast(I32))
+        nc.sync.dma_start(out=w4_w[:], in_=w4_words.rearrange("b p n i -> p b (n i)").bitcast(I32))
+
+        nc.gpsimd.memset(zero[:], 0.0)
+        nc.vector.memset(tab_s[:].bitcast(I32), 0)
+        for q in range(QUADS):
+            nc.vector.tensor_copy(out=tab_s[live[q], :].bitcast(I32), in_=tab_rows[live[q], :])
+
+        make_identity(nc, ident[:])
+        nc.scalar.activation(out=zero_bias[:], in_=zero[:], func=ACT.Tanh)
+
+        blocks = S // P
+        turned = wgs_turned[:].rearrange("j (u t q s) -> j u t q s", u=blocks, t=PACK, q=QUADS)
+        for u in range(blocks):
+            nc.tensor.transpose(banks[4][:, u * P : (u + 1) * P], wgs_rows[:, u * P : (u + 1) * P], ident[:])
+        for u in range(blocks):
+            src = banks[4][:, u * P : (u + 1) * P].rearrange("j (s t) -> j t s", t=PACK)
+            nc.scalar.copy(out=turned[:, u], in_=src.unsqueeze(2).to_broadcast([P, PACK, QUADS, 32]))
+        for t in range(PACK):
+            for u in range(blocks):
+                c0 = (u * PACK + t) * P
+                nc.tensor.transpose(banks[t][:, u * P : (u + 1) * P], wgs_turned[:, c0 : c0 + P], ident[:])
+        for t in range(PACK):
+            for b in range(H_PASSES):
+                nc.scalar.activation(out=factor[b][t][:], in_=banks[t][:], func=ACT.Copy, scale=gain_c[:, b, t : t + 1])
+
+        def group_w1(copy, b, a, dst):
+            copy(
+                out=dst[:].rearrange("p (t m j) -> p m j t", t=PACK, j=PACK),
+                in_=w1_raw[b][a].rearrange("p (j m t) -> p m j t", j=PACK, t=PACK),
+            )
+
+        def quantize(words, scales, src):
+            nc.vector.quantize_mx(out=words.bitcast(FP8X4), scales=scales, in_=src)
+
+        def first_product(b, a, t, bank):
+            cols = slice(t * P, (t + 1) * P)
+            nc.tensor.matmul_mx(
+                out=bank[:],
+                lhsT=w1_w[b][a][:, cols].bitcast(FP8X4),
+                lhsT_scale=w1_s[b][a][:, cols],
+                rhs=v_w[a][:].bitcast(FP8X4),
+                rhs_scale=v_s[4 * a : P, :],
+                start=(a == 0),
+                stop=(a == K_PASSES - 1),
+            )
+
+        def scatter(b, t, bank):
+            nc.scalar.activation(out=tanh_e[t][:], in_=bank[:], func=ACT.Tanh, bias=zero_bias[:, 0:1])
+            nc.vector.tensor_tensor(page[b][t][:].indirect(list2[:]), tanh_e[t][:], factor[b][t][:], ALU.mult)
+
+        def interleave(copy, dst, src, rows):
+            copy(
+                out=dst.rearrange("p (c i t) -> p c t i", i=4, t=rows),
+                in_=src.rearrange("p t (c i) -> p c t i", i=4),
+            )
+
+        for a in range(K_PASSES):
+            group_w1(nc.vector.tensor_copy, 0, a, stage[a % 2])
+            quantize(w1_w[0][a][:], w1_s[0][a][:], stage[a % 2][:])
+        nc.vector.tensor_copy(v_s[:], tab_s[:].indirect(list1[:]))
+        v_w.append(tile("v_w_last", [P, S], U32, tag="tab_s"))
+        for a in range(K_PASSES):
+            nc.vector.tensor_copy(v_w[a][:], tab_w[a][:].bitcast(U32).indirect(list1[:]))
+            for t in range(PACK):
+                first_product(0, a, t, banks[4 + t])
+        for t in range(PACK):
+            scatter(0, t, banks[4 + t])
+
+        for a in range(K_PASSES):
+            late = tile(f"late{a}", [P, CHUNK], BF16, tag=f"factor0{a}")
+            group_w1(nc.scalar.copy, 1, a, late)
+            quantize(w1_w[1][a][:], w1_s[1][a][:], late[:])
+            for t in range(PACK):
+                first_product(1, a, t, banks[t])
+
+        def gather(b, t):
+            nc.vector.tensor_copy(picked[b][:, t * M : (t + 1) * M], page[b][t][:].indirect(list3[:]))
+
+        def add_bias(b, t):
+            nc.scalar.activation(
+                out=stage[0][:, t * M : (t + 1) * M], in_=picked[b][:, t * M : (t + 1) * M],
+                func=ACT.Identity, bias=bx_c[:, b, t : t + 1],
+            )
+
+        def join(b, t):
+            nc.sync.dma_start(out=joined[b][:, t * T2 : (t + 1) * T2], in_=page[b][t][:])
+
+        def store_page(b, t):
+            nc.sync.dma_start(out=page_out[b, t], in_=page[b][t][:])
+
+        def group_page(b, part, parts):
+            w = T2 // parts
+            src = joined[b].rearrange("p (t m) -> p t m", t=PACK)[:, :, part * w : (part + 1) * w]
+            interleave(nc.scalar.copy, page_bf[:, part * w * PACK : (part + 1) * w * PACK], src, PACK)
+
+        def quantize_page(b, half):
+            w = T2 // 2
+            cols = slice(half * w, (half + 1) * w)
+            quantize(plane_w[b][:, cols], plane_s[:, b, cols], page_bf[:, half * w * PACK : (half + 1) * w * PACK])
+
+        def store_plane(b):
+            nc.sync.dma_start(out=out_2[b].rearrange("p m i -> p (m i)").bitcast(I32), in_=plane_w[b][:].bitcast(I32))
+
+        def second_product(which, n, b, bank):
+            cols = slice(n * P, (n + 1) * P)
+            if which == 0:
+                wide = slice(b * N + n * P, b * N + (n + 1) * P)
+                words, scales = w2_w[:, wide].bitcast(FP8X4), w2_s[:, wide]
+            elif which == 1:
+                words, scales = w3_w[:, b, 2 * n * P : 2 * (n + 1) * P].bitcast(FP4X4), w3_s[:, b, cols]
+            else:
+                words, scales = w4_w[:, b, cols].bitcast(FP8X4), w4_s[:, b, cols]
+            nc.tensor.matmul_mx(
+                out=bank[:], lhsT=words, lhsT_scale=scales, rhs=x_w[b][:].bitcast(FP8X4), rhs_scale=x_s[b][:],
+                start=(b == 0), stop=(b == H_PASSES - 1),
+            )
+
+        for t in range(PACK):
+            join(0, t)
+        for t in range(PACK):
+            gather(0, t)
+        for t in range(PACK):
+            scatter(1, t, banks[t])
+        for t in range(PACK - 1):
+            join(1, t)
+        for b in range(H_PASSES):
+            for t in range(PACK):
+                store_page(b, t)
+
+        for b in range(H_PASSES):
+            interleave(nc.scalar.copy, w2_bf[:, b * N * PACK : (b + 1) * N * PACK], w2_raw[b][:], PACK)
+        quantize(w2_w[:, 0:512], w2_s[:, 0:512], w2_bf[:, 0:2048])
+        quantize(w2_w[:, 512:768], w2_s[:, 512:768], w2_bf[:, 2048:3072])
+
+        for t in range(PACK):
+            add_bias(0, t)
+        interleave(nc.scalar.copy, stage[1][:], stage[0][:].rearrange("p (t m) -> p t m", t=PACK), PACK)
+        quantize(x_w[0][:], x_s[0][:], stage[1][:])
+        sums = [(n, which) for n in range(N_TILES) for which in range(3)]
+        for i, (n, which) in enumerate(sums[:8]):
+            second_product(which, n, 0, banks[i])
+        for half in range(2):
+            group_page(0, half, 2)
+            quantize_page(0, half)
+        store_plane(0)
+
+        for t in range(PACK):
+            gather(1, t)
+        last = PACK - 1
+        nc.scalar.copy(out=joined[1][:, last * T2 : (last + 1) * T2], in_=page[1][last][:])
+        group_page(1, 0, 4)
+        group_page(1, 1, 4)
+        add_bias(1, 0)
+        add_bias(1, 1)
+        group_page(1, 2, 4)
+        add_bias(1, 2)
+        add_bias(1, 3)
+        group_page(1, 3, 4)
+        interleave(nc.vector.tensor_copy, stage[1][:], stage[0][:].rearrange("p (t m) -> p t m", t=PACK), PACK)
+        quantize(x_w[1][:], x_s[1][:], stage[1][:])
+        for i, (n, which) in enumerate(sums[:8]):
+            second_product(which, n, 1, banks[i])
+        for half in range(2):
+            quantize_page(1, half)
+        store_plane(1)
+        for q in range(QUADS):
+            nc.sync.dma_start(
+                out=out_3[:, 4 * q : 4 * q + 4, :].rearrange("b r m -> r b m").bitcast(I32),
+                in_=plane_s[32 * q : 32 * q + 4, :, :].bitcast(I32),
+            )
+
+        for n in range(N_TILES):
+            y2 = wgs_turned[:, n * M : (n + 1) * M]
+            prod = factor[1][n]
+            y = tanh_e[n]
+            nc.scalar.copy(out=y2, in_=banks[3 * n][:])
+            if n == 0:
+                for b in range(H_PASSES):
+                    second_product(2, N_TILES - 1, b, banks[0])
+            y4 = banks[(3 * n + 2) % 8]
+            nc.vector.tensor_tensor(prod[:], banks[3 * n + 1][:], y2, ALU.mult)
+            nc.vector.tensor_tensor(y[:], y4[:], prod[:], ALU.add)
+            nc.sync.dma_start(out=out_0[n * P : (n + 1) * P, :], in_=y[:])

@@ -97,13 +97,13 @@ def tile_list_hint_slot_features_kernel(
 
         nc.sync.dma_start(out=wgs_rows[:], in_=wgs)
         load_w1(0, 0)
-        load_w1(0, 1)
         live = [slice(32 * q, 32 * q + 4 * K_PASSES) for q in range(QUADS)]
         for q in range(QUADS):
             nc.sync.dma_start(out=tab_rows[live[q], :], in_=tab_scales[:, 4 * q : 4 * q + 4, :].bitcast(I32))
+        load_w1(0, 1)
+        load_w1(0, 2)
         nc.sync.dma_start(out=gain_c[:], in_=gain.rearrange("(b p t) -> p b t", p=P, t=PACK))
         nc.sync.dma_start(list1[:], offs)
-        load_w1(0, 2)
         for a in range(K_PASSES):
             nc.sync.dma_start(out=tab_w[a][:], in_=tab_words[a].rearrange("p t i -> p (t i)").bitcast(I32))
         nc.sync.dma_start(list2[:], offs2)
@@ -152,28 +152,33 @@ def tile_list_hint_slot_features_kernel(
 
         def group_w1(copy, b, a, dst):
             copy(
-                out=dst[:].rearrange("p (t m j) -> p m j t", t=PACK, j=PACK),
-                in_=w1_raw[b][a].rearrange("p (j m t) -> p m j t", j=PACK, t=PACK),
+                out=dst[:].rearrange("p (u v m j) -> p u m j v", u=2, v=2, j=PACK),
+                in_=w1_raw[b][a].rearrange("p (j m u v) -> p u m j v", j=PACK, u=2, v=2),
             )
 
         def quantize(words, scales, src):
             nc.vector.quantize_mx(out=words.bitcast(FP8X4), scales=scales, in_=src)
 
-        def first_product(b, a, t, bank):
+        def first_product(b, a, t, bank, part=slice(0, S)):
             cols = slice(t * P, (t + 1) * P)
             nc.tensor.matmul_mx(
-                out=bank[:],
+                out=bank[:, part],
                 lhsT=w1_w[b][a][:, cols].bitcast(FP8X4),
                 lhsT_scale=w1_s[b][a][:, cols],
-                rhs=v_w[a][:].bitcast(FP8X4),
-                rhs_scale=v_s[4 * a : P, :],
+                rhs=v_w[a][:, part].bitcast(FP8X4),
+                rhs_scale=v_s[4 * a : P, part],
                 start=(a == 0),
                 stop=(a == K_PASSES - 1),
             )
 
-        def scatter(b, t, bank):
-            nc.scalar.activation(out=tanh_e[t][:], in_=bank[:], func=ACT.Tanh, bias=zero_bias[:, 0:1])
-            nc.vector.tensor_tensor(page[b][t][:].indirect(list2[:]), tanh_e[t][:], factor[b][t][:], ALU.mult)
+        def entries(offsets, part):
+            return offsets[:, part.start // 16 : part.stop // 16]
+
+        def scatter(b, t, bank, part=slice(0, S)):
+            nc.scalar.activation(out=tanh_e[t][:, part], in_=bank[:, part], func=ACT.Tanh, bias=zero_bias[:, 0:1])
+            nc.vector.tensor_tensor(
+                page[b][t][:].indirect(entries(list2, part)), tanh_e[t][:, part], factor[b][t][:, part], ALU.mult
+            )
 
         def interleave(copy, dst, src, rows):
             copy(
@@ -186,11 +191,18 @@ def tile_list_hint_slot_features_kernel(
             quantize(w1_w[0][a][:], w1_s[0][a][:], stage[a % 2][:])
         nc.vector.tensor_copy(v_s[:], tab_s[:].indirect(list1[:]))
         v_w.append(tile("v_w_last", [P, S], U32, tag="tab_s"))
+        halves = [slice(0, S // 2), slice(S // 2, S)]
+        half_banks = [banks[4], banks[0]]
         for a in range(K_PASSES):
-            nc.vector.tensor_copy(v_w[a][:], tab_w[a][:].bitcast(U32).indirect(list1[:]))
-            for t in range(PACK):
+            for part in halves if a == K_PASSES - 1 else [slice(0, S)]:
+                nc.vector.tensor_copy(v_w[a][:, part], tab_w[a][:].bitcast(U32).indirect(entries(list1, part)))
+            for part, bank in zip(halves, half_banks):
+                first_product(0, a, 0, bank, part)
+            for t in range(1, PACK):
                 first_product(0, a, t, banks[4 + t])
-        for t in range(PACK):
+        for part, bank in zip(halves, half_banks):
+            scatter(0, 0, bank, part)
+        for t in range(1, PACK):
             scatter(0, t, banks[4 + t])
 
         for a in range(K_PASSES):
@@ -244,15 +256,17 @@ def tile_list_hint_slot_features_kernel(
 
         for t in range(PACK):
             join(0, t)
+        for t in range(PACK - 1):
+            store_page(0, t)
         for t in range(PACK):
             gather(0, t)
         for t in range(PACK):
             scatter(1, t, banks[t])
         for t in range(PACK - 1):
             join(1, t)
-        for b in range(H_PASSES):
-            for t in range(PACK):
-                store_page(b, t)
+        store_page(0, PACK - 1)
+        for t in range(PACK):
+            store_page(1, t)
 
         for b in range(H_PASSES):
             interleave(nc.scalar.copy, w2_bf[:, b * N * PACK : (b + 1) * N * PACK], w2_raw[b][:], PACK)
@@ -261,18 +275,19 @@ def tile_list_hint_slot_features_kernel(
 
         for t in range(PACK):
             add_bias(0, t)
-        interleave(nc.scalar.copy, stage[1][:], stage[0][:].rearrange("p (t m) -> p t m", t=PACK), PACK)
-        quantize(x_w[0][:], x_s[0][:], stage[1][:])
-        sums = [(n, which) for n in range(N_TILES) for which in range(3)]
-        for i, (n, which) in enumerate(sums[:8]):
-            second_product(which, n, 0, banks[i])
         for half in range(2):
             group_page(0, half, 2)
             quantize_page(0, half)
         store_plane(0)
+        x0_bf = joined[0][:, T2 : 2 * T2].bitcast(BF16)
+        interleave(nc.scalar.copy, x0_bf, stage[0][:].rearrange("p (t m) -> p t m", t=PACK), PACK)
 
         for t in range(PACK):
             gather(1, t)
+        quantize(x_w[0][:], x_s[0][:], x0_bf)
+        sums = [(n, which) for n in range(N_TILES) for which in range(3)]
+        for i, (n, which) in enumerate(sums[:8]):
+            second_product(which, n, 0, banks[i])
         last = PACK - 1
         nc.scalar.copy(out=joined[1][:, last * T2 : (last + 1) * T2], in_=page[1][last][:])
         group_page(1, 0, 4)

@@ -21,10 +21,20 @@ P = 128
 PACK = 4
 PASS = P * PACK
 K_PASSES = K // PASS
-H_PASSES = H // PASS
+GROUPS = H // PASS
 N_TILES = N // P
 QUADS = 4
+QUAD = P // QUADS
+SCALE_ROWS = 4
+PER_COLUMN = 16
+BANK = 512
+BANKS = 8
+HALF = M // 2
 CHUNK = PACK * PASS
+RUN = 4
+W2_SPLIT = 512
+PAGE_CUTS = (0, 512, 640, 768, 1024)
+W2, W3, W4 = 0, 1, 2
 
 
 def tile_list_hint_slot_features_kernel(
@@ -39,52 +49,51 @@ def tile_list_hint_slot_features_kernel(
         def tile(name, shape, dtype, tag=None):
             return sb.tile(shape, dtype, name=name, tag=tag or name, align_bytes=64)
 
-        banks = [ps.tile([P, 512], F32, name=f"bank{i}") for i in range(8)]
+        banks = [ps.tile([P, BANK], F32, name=f"bank{i}") for i in range(BANKS)]
 
-        list1 = tile("list1", [P, S // 16], U16)
-        list2 = tile("list2", [P, S // 16], U16)
-        list3 = tile("list3", [P, M // 16], U16)
+        list1 = tile("list1", [P, S // PER_COLUMN], U16)
+        list2 = tile("list2", [P, S // PER_COLUMN], U16)
+        list3 = tile("list3", [P, M // PER_COLUMN], U16)
         tab_w = [tile(f"tab_w{a}", [P, T], I32) for a in range(K_PASSES)]
-        tab_rows = tile("tab_rows", [P, T // 4], I32)
         tab_s = tile("tab_s", [P, T], U8)
-        v_w = [tile(f"v_w{a}", [P, S], U32) for a in range(K_PASSES - 1)]
         v_s = tile("v_s", [P, S], U8)
-        work = tile("work", [P, H_PASSES * K_PASSES * CHUNK], F32)
-        page = [[tile(f"page{b}{t}", [P, T2], F32) for t in range(PACK)] for b in range(H_PASSES)]
+        work = tile("work", [P, GROUPS * K_PASSES * CHUNK], F32)
+        page = [[tile(f"page{b}{t}", [P, T2], F32) for t in range(PACK)] for b in range(GROUPS)]
         wgs_rows = tile("wgs_rows", [P, S], F32)
         wgs_turned = tile("wgs_turned", [P, S // P * PACK * P], F32)
-        factor = [[tile(f"factor{b}{t}", [P, S], F32) for t in range(PACK)] for b in range(H_PASSES)]
+        factor = [[tile(f"factor{b}{t}", [P, S], F32) for t in range(PACK)] for b in range(GROUPS)]
         tanh_e = [tile(f"tanh_e{t}", [P, S], F32) for t in range(PACK)]
-        gain_c = tile("gain_c", [P, H_PASSES, PACK], F32)
-        bx_c = tile("bx_c", [P, H_PASSES, PACK], F32)
-        w2_raw = [tile(f"w2_raw{b}", [P, PACK, N], F32) for b in range(H_PASSES)]
-        w2_w = tile("w2_w", [P, H_PASSES * N], U32)
-        w2_s = tile("w2_s", [P, H_PASSES * N], U8)
-        w3_w = tile("w3_w", [P, H_PASSES, 2 * N], U8)
-        w3_s = tile("w3_s", [P, H_PASSES, N], U8)
-        w4_w = tile("w4_w", [P, H_PASSES, N], I32)
-        w4_s = tile("w4_s", [P, H_PASSES, N], U8)
+        gain_c = tile("gain_c", [P, GROUPS, PACK], F32)
+        bx_c = tile("bx_c", [P, GROUPS, PACK], F32)
+        w2_raw = [tile(f"w2_raw{b}", [P, PACK, N], F32) for b in range(GROUPS)]
+        w2_w = tile("w2_w", [P, GROUPS * N], U32)
+        w2_s = tile("w2_s", [P, GROUPS * N], U8)
+        w3_w = tile("w3_w", [P, GROUPS, 2 * N], U8)
+        w3_s = tile("w3_s", [P, GROUPS, N], U8)
+        w4_w = tile("w4_w", [P, GROUPS, N], I32)
+        w4_s = tile("w4_s", [P, GROUPS, N], U8)
         ident = tile("ident", [P, P], F32)
-        zero = tile("zero", [P, 8], F32)
-        zero_bias = tile("zero_bias", [P, 8], F32)
+        zero = tile("zero", [P, 1], F32)
+        zero_bias = tile("zero_bias", [P, 1], F32)
         stage = [tile(f"stage{i}", [P, CHUNK], BF16) for i in range(2)]
-        w1_w = [[tile(f"w1_w{b}{a}", [P, PASS], U32) for a in range(K_PASSES)] for b in range(H_PASSES)]
-        w1_s = [[tile(f"w1_s{b}{a}", [P, PASS], U8) for a in range(K_PASSES)] for b in range(H_PASSES)]
-        x_w = [tile(f"x_w{b}", [P, M], U32) for b in range(H_PASSES)]
-        x_s = [tile(f"x_s{b}", [P, M], U8) for b in range(H_PASSES)]
-        page_bf = tile("page_bf", [P, T2 * PACK], BF16)
-        plane_w = [tile(f"plane_w{b}", [P, T2], U32) for b in range(H_PASSES)]
-        plane_s = tile("plane_s", [P, H_PASSES, T2], U8)
+        w1_w = [[tile(f"w1_w{b}{a}", [P, PASS], U32) for a in range(K_PASSES)] for b in range(GROUPS)]
+        w1_s = [[tile(f"w1_s{b}{a}", [P, PASS], U8) for a in range(K_PASSES)] for b in range(GROUPS)]
+        x_w = [tile(f"x_w{b}", [P, M], U32) for b in range(GROUPS)]
+        x_s = [tile(f"x_s{b}", [P, M], U8) for b in range(GROUPS)]
+        page0_bf = tile("page0_bf", [P, T2 * PACK], BF16)
+        plane_w = [tile(f"plane_w{b}", [P, T2], U32) for b in range(GROUPS)]
+        plane_s = [tile(f"plane_s{b}", [P, T2], U8) for b in range(GROUPS)]
 
-        def chunk(i, count=1):
-            return work[:, i * CHUNK : (i + count) * CHUNK]
+        w1_raw = [
+            [work[:, (b * K_PASSES + a) * CHUNK : (b * K_PASSES + a + 1) * CHUNK] for a in range(K_PASSES)]
+            for b in range(GROUPS)
+        ]
+        joined = [work[:, (PACK - 1) * T2 : (2 * PACK - 1) * T2], work[:, 0 : PACK * T2]]
+        w2_bf = w1_raw[1][1].bitcast(BF16)
+        picked0 = w1_raw[1][2]
+        page_bf = [page0_bf[:], w1_raw[1][2].bitcast(BF16)]
 
-        w1_raw = [[chunk(b * K_PASSES + a) for a in range(K_PASSES)] for b in range(H_PASSES)]
-        joined = [work[:, 3 * T2 : 7 * T2], work[:, 0 : 4 * T2]]
-        w2_bf = chunk(4).bitcast(BF16)
-        picked = [chunk(5), work[:, 5 * T2 : 7 * T2]]
-
-        w1_rows = w1.rearrange("(a p j) (b c) -> b a p j c", p=P, j=PACK, b=H_PASSES)
+        w1_rows = w1.rearrange("(a p j) (b c) -> b a p j c", p=P, j=PACK, b=GROUPS)
         page_in = page0.rearrange("(b p t) m -> b t p m", p=P, t=PACK)
         page_out = out_1.rearrange("(b p t) m -> b t p m", p=P, t=PACK)
         w2_rows = w2.rearrange("(b p j) n -> b p j n", p=P, j=PACK)
@@ -95,15 +104,15 @@ def tile_list_hint_slot_features_kernel(
         def load_page(b, t):
             nc.sync.dma_start(out=page[b][t][:], in_=page_in[b, t])
 
+        def block_rows(q):
+            return slice(SCALE_ROWS * q, SCALE_ROWS * (q + 1))
+
         nc.sync.dma_start(out=wgs_rows[:], in_=wgs)
         load_w1(0, 0)
-        live = [slice(32 * q, 32 * q + 4 * K_PASSES) for q in range(QUADS)]
-        for q in range(QUADS):
-            nc.sync.dma_start(out=tab_rows[live[q], :], in_=tab_scales[:, 4 * q : 4 * q + 4, :].bitcast(I32))
-        load_w1(0, 1)
-        load_w1(0, 2)
         nc.sync.dma_start(out=gain_c[:], in_=gain.rearrange("(b p t) -> p b t", p=P, t=PACK))
+        load_w1(0, 1)
         nc.sync.dma_start(list1[:], offs)
+        load_w1(0, 2)
         for a in range(K_PASSES):
             nc.sync.dma_start(out=tab_w[a][:], in_=tab_words[a].rearrange("p t i -> p (t i)").bitcast(I32))
         nc.sync.dma_start(list2[:], offs2)
@@ -111,18 +120,18 @@ def tile_list_hint_slot_features_kernel(
         for a in range(K_PASSES):
             load_page(0, a + 1)
             load_w1(1, a)
-        for b in range(H_PASSES):
+        for b in range(GROUPS):
             nc.sync.dma_start(out=w2_raw[b][:], in_=w2_rows[b])
         nc.sync.dma_start(list3[:], offs3)
         nc.sync.dma_start(out=bx_c[:], in_=bx.rearrange("(b p t) -> p b t", p=P, t=PACK))
-        for plane in (w3_s, w4_s):
-            nc.gpsimd.memset(plane[:].bitcast(I32), 0)
+        for scale_tile in (w3_s, w4_s):
+            nc.gpsimd.memset(scale_tile[:].bitcast(I32), 0)
         for q in range(QUADS):
             load_page(1, q)
-            for plane, rows in ((w3_s, w3_scales), (w4_s, w4_scales)):
+            for scale_tile, rows in ((w3_s, w3_scales), (w4_s, w4_scales)):
                 nc.sync.dma_start(
-                    out=plane[32 * q : 32 * q + 4, :, :].bitcast(I32),
-                    in_=rows[:, 4 * q : 4 * q + 4, :].rearrange("b r n -> r b n").bitcast(I32),
+                    out=scale_tile[QUAD * q : QUAD * q + SCALE_ROWS, :, :].bitcast(I32),
+                    in_=rows[:, block_rows(q), :].rearrange("b r n -> r b n").bitcast(I32),
                 )
         nc.sync.dma_start(out=w3_w[:].bitcast(I32), in_=w3_words.rearrange("b p c -> p b c").bitcast(I32))
         nc.sync.dma_start(out=w4_w[:], in_=w4_words.rearrange("b p n i -> p b (n i)").bitcast(I32))
@@ -130,7 +139,10 @@ def tile_list_hint_slot_features_kernel(
         nc.gpsimd.memset(zero[:], 0.0)
         nc.vector.memset(tab_s[:].bitcast(I32), 0)
         for q in range(QUADS):
-            nc.vector.tensor_copy(out=tab_s[live[q], :].bitcast(I32), in_=tab_rows[live[q], :])
+            nc.gpsimd.dma_start(
+                out=tab_s[QUAD * q : QUAD * q + SCALE_ROWS * K_PASSES, :].bitcast(I32),
+                in_=tab_scales[:, block_rows(q), :].bitcast(I32),
+            )
 
         make_identity(nc, ident[:])
         nc.scalar.activation(out=zero_bias[:], in_=zero[:], func=ACT.Tanh)
@@ -138,22 +150,22 @@ def tile_list_hint_slot_features_kernel(
         blocks = S // P
         turned = wgs_turned[:].rearrange("j (u t q s) -> j u t q s", u=blocks, t=PACK, q=QUADS)
         for u in range(blocks):
-            nc.tensor.transpose(banks[4][:, u * P : (u + 1) * P], wgs_rows[:, u * P : (u + 1) * P], ident[:])
+            nc.tensor.transpose(banks[PACK][:, u * P : (u + 1) * P], wgs_rows[:, u * P : (u + 1) * P], ident[:])
         for u in range(blocks):
-            src = banks[4][:, u * P : (u + 1) * P].rearrange("j (s t) -> j t s", t=PACK)
-            nc.scalar.copy(out=turned[:, u], in_=src.unsqueeze(2).to_broadcast([P, PACK, QUADS, 32]))
+            src = banks[PACK][:, u * P : (u + 1) * P].rearrange("j (s t) -> j t s", t=PACK)
+            nc.scalar.copy(out=turned[:, u], in_=src.unsqueeze(2).to_broadcast([P, PACK, QUADS, QUAD]))
         for t in range(PACK):
             for u in range(blocks):
                 c0 = (u * PACK + t) * P
                 nc.tensor.transpose(banks[t][:, u * P : (u + 1) * P], wgs_turned[:, c0 : c0 + P], ident[:])
         for t in range(PACK):
-            for b in range(H_PASSES):
+            for b in range(GROUPS):
                 nc.scalar.activation(out=factor[b][t][:], in_=banks[t][:], func=ACT.Copy, scale=gain_c[:, b, t : t + 1])
 
-        def group_w1(copy, b, a, dst):
+        def round_w1(copy, b, a, dst):
             copy(
-                out=dst[:].rearrange("p (u v m j) -> p u m j v", u=2, v=2, j=PACK),
-                in_=w1_raw[b][a].rearrange("p (j m u v) -> p u m j v", j=PACK, u=2, v=2),
+                out=dst[:].rearrange("p (u v c j) -> p u c j v", u=2, v=2, j=PACK),
+                in_=w1_raw[b][a].rearrange("p (j c u v) -> p u c j v", j=PACK, u=2, v=2),
             )
 
         def quantize(words, scales, src):
@@ -166,160 +178,186 @@ def tile_list_hint_slot_features_kernel(
                 lhsT=w1_w[b][a][:, cols].bitcast(FP8X4),
                 lhsT_scale=w1_s[b][a][:, cols],
                 rhs=v_w[a][:, part].bitcast(FP8X4),
-                rhs_scale=v_s[4 * a : P, part],
+                rhs_scale=v_s[SCALE_ROWS * a : P, part],
                 start=(a == 0),
                 stop=(a == K_PASSES - 1),
             )
 
         def entries(offsets, part):
-            return offsets[:, part.start // 16 : part.stop // 16]
+            return offsets[:, part.start // PER_COLUMN : part.stop // PER_COLUMN]
 
         def scatter(b, t, bank, part=slice(0, S)):
-            nc.scalar.activation(out=tanh_e[t][:, part], in_=bank[:, part], func=ACT.Tanh, bias=zero_bias[:, 0:1])
+            nc.scalar.activation(out=tanh_e[t][:, part], in_=bank[:, part], func=ACT.Tanh, bias=zero_bias[:])
             nc.vector.tensor_tensor(
                 page[b][t][:].indirect(entries(list2, part)), tanh_e[t][:, part], factor[b][t][:, part], ALU.mult
             )
 
-        def interleave(copy, dst, src, rows):
+        def interleave(copy, dst, src):
             copy(
-                out=dst.rearrange("p (c i t) -> p c t i", i=4, t=rows),
-                in_=src.rearrange("p t (c i) -> p c t i", i=4),
+                out=dst.rearrange("p (c i t) -> p c t i", i=RUN, t=PACK),
+                in_=src.rearrange("p t (c i) -> p c t i", i=RUN),
             )
 
         for a in range(K_PASSES):
-            group_w1(nc.vector.tensor_copy, 0, a, stage[a % 2])
+            round_w1(nc.vector.tensor_copy, 0, a, stage[a % 2])
             quantize(w1_w[0][a][:], w1_s[0][a][:], stage[a % 2][:])
         nc.vector.tensor_copy(v_s[:], tab_s[:].indirect(list1[:]))
-        v_w.append(tile("v_w_last", [P, S], U32, tag="tab_s"))
-        halves = [slice(0, S // 2), slice(S // 2, S)]
-        half_banks = [banks[4], banks[0]]
+        v_w = [tile(f"v_w{a}", [P, S], U32, tag="tab_s" if a == 0 else None) for a in range(K_PASSES)]
+        list_halves = [slice(0, S // 2), slice(S // 2, S)]
+        half_banks = [banks[PACK], banks[0]]
         for a in range(K_PASSES):
-            for part in halves if a == K_PASSES - 1 else [slice(0, S)]:
+            for part in list_halves if a == K_PASSES - 1 else [slice(0, S)]:
                 nc.vector.tensor_copy(v_w[a][:, part], tab_w[a][:].bitcast(U32).indirect(entries(list1, part)))
-            for part, bank in zip(halves, half_banks):
+            for part, bank in zip(list_halves, half_banks):
                 first_product(0, a, 0, bank, part)
             for t in range(1, PACK):
-                first_product(0, a, t, banks[4 + t])
-        for part, bank in zip(halves, half_banks):
+                first_product(0, a, t, banks[PACK + t])
+        for part, bank in zip(list_halves, half_banks):
             scatter(0, 0, bank, part)
         for t in range(1, PACK):
-            scatter(0, t, banks[4 + t])
+            scatter(0, t, banks[PACK + t])
 
         for a in range(K_PASSES):
             late = tile(f"late{a}", [P, CHUNK], BF16, tag=f"factor0{a}")
-            group_w1(nc.scalar.copy, 1, a, late)
+            round_w1(nc.scalar.copy, 1, a, late)
             quantize(w1_w[1][a][:], w1_s[1][a][:], late[:])
             for t in range(PACK):
                 first_product(1, a, t, banks[t])
 
-        def gather(b, t):
-            nc.vector.tensor_copy(picked[b][:, t * M : (t + 1) * M], page[b][t][:].indirect(list3[:]))
+        def gather(b, t, dst, part):
+            nc.vector.tensor_copy(dst[:, t, :], page[b][t][:].indirect(entries(list3, part)))
 
-        def add_bias(b, t):
-            nc.scalar.activation(
-                out=stage[0][:, t * M : (t + 1) * M], in_=picked[b][:, t * M : (t + 1) * M],
-                func=ACT.Identity, bias=bx_c[:, b, t : t + 1],
-            )
+        def add_bias(b, t, dst, src):
+            nc.scalar.activation(out=dst[:, t, :], in_=src[:, t, :], func=ACT.Identity, bias=bx_c[:, b, t : t + 1])
 
-        def join(b, t):
-            nc.sync.dma_start(out=joined[b][:, t * T2 : (t + 1) * T2], in_=page[b][t][:])
+        def by_slice(ap):
+            return ap.rearrange("p (t m) -> p t m", t=PACK)
+
+        def join(b, t, move=nc.sync.dma_start):
+            move(out=joined[b][:, t * T2 : (t + 1) * T2], in_=page[b][t][:])
 
         def store_page(b, t):
             nc.sync.dma_start(out=page_out[b, t], in_=page[b][t][:])
 
-        def group_page(b, part, parts):
-            w = T2 // parts
-            src = joined[b].rearrange("p (t m) -> p t m", t=PACK)[:, :, part * w : (part + 1) * w]
-            interleave(nc.scalar.copy, page_bf[:, part * w * PACK : (part + 1) * w * PACK], src, PACK)
+        def round_page(b, c0, c1):
+            interleave(nc.scalar.copy, page_bf[b][:, c0 * PACK : c1 * PACK], by_slice(joined[b])[:, :, c0:c1])
 
-        def quantize_page(b, half):
+        def quantize_page(b, side):
             w = T2 // 2
-            cols = slice(half * w, (half + 1) * w)
-            quantize(plane_w[b][:, cols], plane_s[:, b, cols], page_bf[:, half * w * PACK : (half + 1) * w * PACK])
+            cols = slice(side * w, (side + 1) * w)
+            quantize(plane_w[b][:, cols], plane_s[b][:, cols], page_bf[b][:, side * w * PACK : (side + 1) * w * PACK])
 
-        def store_plane(b):
+        def store_planes(b):
             nc.sync.dma_start(out=out_2[b].rearrange("p m i -> p (m i)").bitcast(I32), in_=plane_w[b][:].bitcast(I32))
+            for q in range(QUADS):
+                nc.sync.dma_start(
+                    out=out_3[b, block_rows(q), :].bitcast(I32),
+                    in_=plane_s[b][QUAD * q : QUAD * q + SCALE_ROWS, :].bitcast(I32),
+                )
 
-        def second_product(which, n, b, bank):
+        def second_product(weight, n, b, half, dst, start, stop):
             cols = slice(n * P, (n + 1) * P)
-            if which == 0:
+            if weight == W2:
                 wide = slice(b * N + n * P, b * N + (n + 1) * P)
                 words, scales = w2_w[:, wide].bitcast(FP8X4), w2_s[:, wide]
-            elif which == 1:
+            elif weight == W3:
                 words, scales = w3_w[:, b, 2 * n * P : 2 * (n + 1) * P].bitcast(FP4X4), w3_s[:, b, cols]
             else:
                 words, scales = w4_w[:, b, cols].bitcast(FP8X4), w4_s[:, b, cols]
-            nc.tensor.matmul_mx(
-                out=bank[:], lhsT=words, lhsT_scale=scales, rhs=x_w[b][:].bitcast(FP8X4), rhs_scale=x_s[b][:],
-                start=(b == 0), stop=(b == H_PASSES - 1),
-            )
+            width = P if weight == W3 else HALF
+            for c0 in range(0, HALF, width):
+                m_cols = slice(half * HALF + c0, half * HALF + c0 + width)
+                nc.tensor.matmul_mx(
+                    out=dst[:, c0 : c0 + width], lhsT=words, lhsT_scale=scales,
+                    rhs=x_w[b][:, m_cols].bitcast(FP8X4), rhs_scale=x_s[b][:, m_cols],
+                    start=(start and c0 == 0), stop=(stop and c0 + width == HALF),
+                )
 
+        bank_sums = [((W2, 0), (W2, 1)), ((W3, 0), (W3, 1)), ((W4, 0), (W4, 1)), ((W2, 2), (W3, 2))]
+        per_half = len(bank_sums)
+
+        def paired_products(b, half):
+            for i, pair in enumerate(bank_sums):
+                for side, (weight, n) in enumerate(pair):
+                    dst = banks[per_half * half + i][:, side * HALF : (side + 1) * HALF]
+                    second_product(weight, n, b, half, dst, b == 0 and side == 0, b == GROUPS - 1 and side == 1)
+
+        last = PACK - 1
         for t in range(PACK):
             join(0, t)
-        for t in range(PACK - 1):
+        for t in range(last):
             store_page(0, t)
         for t in range(PACK):
-            gather(0, t)
+            gather(0, t, by_slice(picked0), slice(0, M))
         for t in range(PACK):
             scatter(1, t, banks[t])
-        for t in range(PACK - 1):
+        for t in range(last):
             join(1, t)
-        store_page(0, PACK - 1)
+        store_page(0, last)
         for t in range(PACK):
             store_page(1, t)
 
-        for b in range(H_PASSES):
-            interleave(nc.scalar.copy, w2_bf[:, b * N * PACK : (b + 1) * N * PACK], w2_raw[b][:], PACK)
-        quantize(w2_w[:, 0:512], w2_s[:, 0:512], w2_bf[:, 0:2048])
-        quantize(w2_w[:, 512:768], w2_s[:, 512:768], w2_bf[:, 2048:3072])
+        for b in range(GROUPS):
+            interleave(nc.scalar.copy, w2_bf[:, b * N * PACK : (b + 1) * N * PACK], w2_raw[b][:])
+        for c0, c1 in ((0, W2_SPLIT), (W2_SPLIT, GROUPS * N)):
+            quantize(w2_w[:, c0:c1], w2_s[:, c0:c1], w2_bf[:, c0 * PACK : c1 * PACK])
 
         for t in range(PACK):
-            add_bias(0, t)
-        for half in range(2):
-            group_page(0, half, 2)
-            quantize_page(0, half)
-        store_plane(0)
+            add_bias(0, t, by_slice(stage[0][:]), by_slice(picked0))
+        for side in range(2):
+            round_page(0, side * T2 // 2, (side + 1) * T2 // 2)
+            quantize_page(0, side)
+        store_planes(0)
         x0_bf = joined[0][:, T2 : 2 * T2].bitcast(BF16)
-        interleave(nc.scalar.copy, x0_bf, stage[0][:].rearrange("p (t m) -> p t m", t=PACK), PACK)
+        interleave(nc.scalar.copy, x0_bf, by_slice(stage[0][:]))
 
+        m_halves = [slice(0, HALF), slice(HALF, M)]
+        picked1 = [by_slice(joined[0][:, 2 * T2 : 3 * T2]), by_slice(joined[0][:, T2 : 2 * T2])]
+        biased1 = [by_slice(stage[0][:, h * PACK * HALF : (h + 1) * PACK * HALF]) for h in range(2)]
+        x1_bf = [stage[1][:, h * PACK * HALF : (h + 1) * PACK * HALF] for h in range(2)]
         for t in range(PACK):
-            gather(1, t)
+            gather(1, t, picked1[0], m_halves[0])
         quantize(x_w[0][:], x_s[0][:], x0_bf)
-        sums = [(n, which) for n in range(N_TILES) for which in range(3)]
-        for i, (n, which) in enumerate(sums[:8]):
-            second_product(which, n, 0, banks[i])
-        last = PACK - 1
-        nc.scalar.copy(out=joined[1][:, last * T2 : (last + 1) * T2], in_=page[1][last][:])
-        group_page(1, 0, 4)
-        group_page(1, 1, 4)
-        add_bias(1, 0)
-        add_bias(1, 1)
-        group_page(1, 2, 4)
-        add_bias(1, 2)
-        add_bias(1, 3)
-        group_page(1, 3, 4)
-        interleave(nc.vector.tensor_copy, stage[1][:], stage[0][:].rearrange("p (t m) -> p t m", t=PACK), PACK)
-        quantize(x_w[1][:], x_s[1][:], stage[1][:])
-        for i, (n, which) in enumerate(sums[:8]):
-            second_product(which, n, 1, banks[i])
         for half in range(2):
-            quantize_page(1, half)
-        store_plane(1)
-        for q in range(QUADS):
-            nc.sync.dma_start(
-                out=out_3[:, 4 * q : 4 * q + 4, :].rearrange("b r m -> r b m").bitcast(I32),
-                in_=plane_s[32 * q : 32 * q + 4, :, :].bitcast(I32),
-            )
+            paired_products(0, half)
+        for t in range(PACK):
+            gather(1, t, picked1[1], m_halves[1])
+        join(1, last, move=nc.scalar.copy)
+        round_page(1, PAGE_CUTS[0], PAGE_CUTS[1])
+        quantize_page(1, 0)
 
-        for n in range(N_TILES):
-            y2 = wgs_turned[:, n * M : (n + 1) * M]
-            prod = factor[1][n]
-            y = tanh_e[n]
-            nc.scalar.copy(out=y2, in_=banks[3 * n][:])
-            if n == 0:
-                for b in range(H_PASSES):
-                    second_product(2, N_TILES - 1, b, banks[0])
-            y4 = banks[(3 * n + 2) % 8]
-            nc.vector.tensor_tensor(prod[:], banks[3 * n + 1][:], y2, ALU.mult)
-            nc.vector.tensor_tensor(y[:], y4[:], prod[:], ALU.add)
-            nc.sync.dma_start(out=out_0[n * P : (n + 1) * P, :], in_=y[:])
+        def finish_x(half, copy):
+            for t in range(PACK):
+                add_bias(1, t, biased1[half], picked1[half])
+            interleave(copy, x1_bf[half], biased1[half])
+            quantize(x_w[1][:, m_halves[half]], x_s[1][:, m_halves[half]], x1_bf[half])
+            paired_products(1, half)
+
+        finish_x(0, nc.scalar.copy)
+        round_page(1, PAGE_CUTS[1], PAGE_CUTS[2])
+        finish_x(1, nc.vector.tensor_copy)
+
+        out_rows = out_0.rearrange("(n p) m -> p n m", p=P)
+
+        def combine(half):
+            y2_bank, y3_bank, y4_bank, n2_bank = banks[per_half * half : per_half * (half + 1)]
+            y2 = wgs_turned[:, half * 2 * BANK : half * 2 * BANK + N_TILES * HALF]
+            prod = factor[1][2 * half : 2 * half + 2]
+            y = tanh_e[2 * half : 2 * half + 2]
+            nc.scalar.copy(out=y2[:, 0:BANK], in_=y2_bank[:])
+            for b in range(GROUPS):
+                second_product(W4, 2, b, half, y2_bank[:, 0:HALF], b == 0, b == GROUPS - 1)
+            nc.scalar.copy(out=y2[:, BANK : BANK + HALF], in_=n2_bank[:, 0:HALF])
+            nc.vector.tensor_tensor(prod[0][:], y3_bank[:], y2[:, 0:BANK], ALU.mult)
+            nc.vector.tensor_tensor(prod[1][:, 0:HALF], n2_bank[:, HALF:BANK], y2[:, BANK : BANK + HALF], ALU.mult)
+            nc.vector.tensor_tensor(y[0][:], y4_bank[:], prod[0][:], ALU.add)
+            nc.sync.dma_start(out=out_rows[:, 0:2, m_halves[half]], in_=y[0][:].rearrange("p (n m) -> p n m", n=2))
+            nc.vector.tensor_tensor(y[1][:, 0:HALF], y2_bank[:, 0:HALF], prod[1][:, 0:HALF], ALU.add)
+            nc.sync.dma_start(out=out_rows[:, 2, m_halves[half]], in_=y[1][:, 0:HALF])
+
+        round_page(1, PAGE_CUTS[2], PAGE_CUTS[3])
+        combine(0)
+        round_page(1, PAGE_CUTS[3], PAGE_CUTS[4])
+        quantize_page(1, 1)
+        store_planes(1)
+        combine(1)

from contextlib import ExitStack

import concourse.mybir as mybir
from concourse.masks import make_identity

K, H, N, T, S, T2, M = 1536, 1024, 384, 2048, 512, 1024, 512
FLOPS = 2 * K * H * S + 3 * 2 * H * N * M

F32 = mybir.dt.float32
BF16 = mybir.dt.bfloat16
I32 = mybir.dt.int32
U32 = mybir.dt.uint32
U16 = mybir.dt.uint16
U8 = mybir.dt.uint8
FP8X4 = mybir.dt.float8_e4m3fn_x4
FP4X4 = mybir.dt.float4_e2m1fn_x4
ACT = mybir.ActivationFunctionType
ALU = mybir.AluOpType

P = 128
PACK = 4
PASS = P * PACK
K_PASSES = K // PASS
GROUPS = H // PASS
N_TILES = N // P
QUADS = 4
QUAD = P // QUADS
SCALE_ROWS = 4
PER_COLUMN = 16
BANK = 512
BANKS = 8
HALF = M // 2
CHUNK = PACK * PASS
RUN = 4
W2_SPLIT = 512
PAGE_CUTS = (0, 512, 640, 768, 1024)
W2, W3, W4 = 0, 1, 2


def tile_list_hint_slot_features_kernel(
    tc, tab_words, tab_scales, offs, offs2, offs3, w1, gain, wgs, page0, bx, w2,
    w3_words, w3_scales, w4_words, w4_scales, out_0, out_1, out_2, out_3,
):
    nc = tc.nc
    with ExitStack() as ctx:
        sb = ctx.enter_context(tc.tile_pool(name="sb", bufs=1))
        ps = ctx.enter_context(tc.psum_pool(name="ps", bufs=1))

        def tile(name, shape, dtype, tag=None):
            return sb.tile(shape, dtype, name=name, tag=tag or name, align_bytes=64)

        banks = [ps.tile([P, BANK], F32, name=f"bank{i}") for i in range(BANKS)]

        list1 = tile("list1", [P, S // PER_COLUMN], U16)
        list2 = tile("list2", [P, S // PER_COLUMN], U16)
        list3 = tile("list3", [P, M // PER_COLUMN], U16)
        tab_w = [tile(f"tab_w{a}", [P, T], I32) for a in range(K_PASSES)]
        tab_s = tile("tab_s", [P, T], U8)
        v_s = tile("v_s", [P, S], U8)
        work = tile("work", [P, GROUPS * K_PASSES * CHUNK], F32)
        page = [[tile(f"page{b}{t}", [P, T2], F32) for t in range(PACK)] for b in range(GROUPS)]
        wgs_rows = tile("wgs_rows", [P, S], F32)
        wgs_turned = tile("wgs_turned", [P, S // P * PACK * P], F32)
        factor = [[tile(f"factor{b}{t}", [P, S], F32) for t in range(PACK)] for b in range(GROUPS)]
        tanh_e = [tile(f"tanh_e{t}", [P, S], F32) for t in range(PACK)]
        gain_c = tile("gain_c", [P, GROUPS, PACK], F32)
        bx_c = tile("bx_c", [P, GROUPS, PACK], F32)
        w2_raw = [tile(f"w2_raw{b}", [P, PACK, N], F32) for b in range(GROUPS)]
        w2_w = tile("w2_w", [P, GROUPS * N], U32)
        w2_s = tile("w2_s", [P, GROUPS * N], U8)
        w3_w = tile("w3_w", [P, GROUPS, 2 * N], U8)
        w3_s = tile("w3_s", [P, GROUPS, N], U8)
        w4_w = tile("w4_w", [P, GROUPS, N], I32)
        w4_s = tile("w4_s", [P, GROUPS, N], U8)
        ident = tile("ident", [P, P], F32)
        zero = tile("zero", [P, 1], F32)
        zero_bias = tile("zero_bias", [P, 1], F32)
        stage = [tile(f"stage{i}", [P, CHUNK], BF16) for i in range(2)]
        w1_w = [[tile(f"w1_w{b}{a}", [P, PASS], U32) for a in range(K_PASSES)] for b in range(GROUPS)]
        w1_s = [[tile(f"w1_s{b}{a}", [P, PASS], U8) for a in range(K_PASSES)] for b in range(GROUPS)]
        x_w = [tile(f"x_w{b}", [P, M], U32) for b in range(GROUPS)]
        x_s = [tile(f"x_s{b}", [P, M], U8) for b in range(GROUPS)]
        page0_bf = tile("page0_bf", [P, T2 * PACK], BF16)
        plane_w = [tile(f"plane_w{b}", [P, T2], U32) for b in range(GROUPS)]
        plane_s = [tile(f"plane_s{b}", [P, T2], U8) for b in range(GROUPS)]

        w1_raw = [
            [work[:, (b * K_PASSES + a) * CHUNK : (b * K_PASSES + a + 1) * CHUNK] for a in range(K_PASSES)]
            for b in range(GROUPS)
        ]
        joined = [work[:, (PACK - 1) * T2 : (2 * PACK - 1) * T2], work[:, 0 : PACK * T2]]
        w2_bf = w1_raw[1][1].bitcast(BF16)
        picked0 = w1_raw[1][2]
        page_bf = [page0_bf[:], w1_raw[1][2].bitcast(BF16)]

        w1_rows = w1.rearrange("(a p j) (b c) -> b a p j c", p=P, j=PACK, b=GROUPS)
        page_in = page0.rearrange("(b p t) m -> b t p m", p=P, t=PACK)
        page_out = out_1.rearrange("(b p t) m -> b t p m", p=P, t=PACK)
        w2_rows = w2.rearrange("(b p j) n -> b p j n", p=P, j=PACK)

        def load_w1(b, a):
            nc.sync.dma_start(out=w1_raw[b][a].rearrange("p (j c) -> p j c", j=PACK), in_=w1_rows[b, a])

        def load_page(b, t):
            nc.sync.dma_start(out=page[b][t][:], in_=page_in[b, t])

        def block_rows(q):
            return slice(SCALE_ROWS * q, SCALE_ROWS * (q + 1))

        nc.sync.dma_start(out=wgs_rows[:], in_=wgs)
        load_w1(0, 0)
        nc.sync.dma_start(out=gain_c[:], in_=gain.rearrange("(b p t) -> p b t", p=P, t=PACK))
        load_w1(0, 1)
        nc.sync.dma_start(list1[:], offs)
        load_w1(0, 2)
        for a in range(K_PASSES):
            nc.sync.dma_start(out=tab_w[a][:], in_=tab_words[a].rearrange("p t i -> p (t i)").bitcast(I32))
        nc.sync.dma_start(list2[:], offs2)
        load_page(0, 0)
        for a in range(K_PASSES):
            load_page(0, a + 1)
            load_w1(1, a)
        for b in range(GROUPS):
            nc.sync.dma_start(out=w2_raw[b][:], in_=w2_rows[b])
        nc.sync.dma_start(list3[:], offs3)
        nc.sync.dma_start(out=bx_c[:], in_=bx.rearrange("(b p t) -> p b t", p=P, t=PACK))
        for scale_tile in (w3_s, w4_s):
            nc.gpsimd.memset(scale_tile[:].bitcast(I32), 0)
        for q in range(QUADS):
            load_page(1, q)
            for scale_tile, rows in ((w3_s, w3_scales), (w4_s, w4_scales)):
                nc.sync.dma_start(
                    out=scale_tile[QUAD * q : QUAD * q + SCALE_ROWS, :, :].bitcast(I32),
                    in_=rows[:, block_rows(q), :].rearrange("b r n -> r b n").bitcast(I32),
                )
        nc.sync.dma_start(out=w3_w[:].bitcast(I32), in_=w3_words.rearrange("b p c -> p b c").bitcast(I32))
        nc.sync.dma_start(out=w4_w[:], in_=w4_words.rearrange("b p n i -> p b (n i)").bitcast(I32))

        nc.gpsimd.memset(zero[:], 0.0)
        nc.vector.memset(tab_s[:].bitcast(I32), 0)
        for q in range(QUADS):
            nc.gpsimd.dma_start(
                out=tab_s[QUAD * q : QUAD * q + SCALE_ROWS * K_PASSES, :].bitcast(I32),
                in_=tab_scales[:, block_rows(q), :].bitcast(I32),
            )

        make_identity(nc, ident[:])
        nc.scalar.activation(out=zero_bias[:], in_=zero[:], func=ACT.Tanh)

        blocks = S // P
        turned = wgs_turned[:].rearrange("j (u t q s) -> j u t q s", u=blocks, t=PACK, q=QUADS)
        for u in range(blocks):
            nc.tensor.transpose(banks[PACK][:, u * P : (u + 1) * P], wgs_rows[:, u * P : (u + 1) * P], ident[:])
        for u in range(blocks):
            src = banks[PACK][:, u * P : (u + 1) * P].rearrange("j (s t) -> j t s", t=PACK)
            nc.scalar.copy(out=turned[:, u], in_=src.unsqueeze(2).to_broadcast([P, PACK, QUADS, QUAD]))
        for t in range(PACK):
            for u in range(blocks):
                c0 = (u * PACK + t) * P
                nc.tensor.transpose(banks[t][:, u * P : (u + 1) * P], wgs_turned[:, c0 : c0 + P], ident[:])
        for t in range(PACK):
            for b in range(GROUPS):
                nc.scalar.activation(out=factor[b][t][:], in_=banks[t][:], func=ACT.Copy, scale=gain_c[:, b, t : t + 1])

        def round_w1(copy, b, a, dst):
            copy(
                out=dst[:].rearrange("p (u v c j) -> p u c j v", u=2, v=2, j=PACK),
                in_=w1_raw[b][a].rearrange("p (j c u v) -> p u c j v", j=PACK, u=2, v=2),
            )

        def quantize(words, scales, src):
            nc.vector.quantize_mx(out=words.bitcast(FP8X4), scales=scales, in_=src)

        def first_product(b, a, t, bank, part=slice(0, S)):
            cols = slice(t * P, (t + 1) * P)
            nc.tensor.matmul_mx(
                out=bank[:, part],
                lhsT=w1_w[b][a][:, cols].bitcast(FP8X4),
                lhsT_scale=w1_s[b][a][:, cols],
                rhs=v_w[a][:, part].bitcast(FP8X4),
                rhs_scale=v_s[SCALE_ROWS * a : P, part],
                start=(a == 0),
                stop=(a == K_PASSES - 1),
            )

        def entries(offsets, part):
            return offsets[:, part.start // PER_COLUMN : part.stop // PER_COLUMN]

        def scatter(b, t, bank, part=slice(0, S)):
            nc.scalar.activation(out=tanh_e[t][:, part], in_=bank[:, part], func=ACT.Tanh, bias=zero_bias[:])
            nc.vector.tensor_tensor(
                page[b][t][:].indirect(entries(list2, part)), tanh_e[t][:, part], factor[b][t][:, part], ALU.mult
            )

        def interleave(copy, dst, src):
            copy(
                out=dst.rearrange("p (c i t) -> p c t i", i=RUN, t=PACK),
                in_=src.rearrange("p t (c i) -> p c t i", i=RUN),
            )

        for a in range(K_PASSES):
            round_w1(nc.vector.tensor_copy, 0, a, stage[a % 2])
            quantize(w1_w[0][a][:], w1_s[0][a][:], stage[a % 2][:])
        nc.vector.tensor_copy(v_s[:], tab_s[:].indirect(list1[:]))
        v_w = [tile(f"v_w{a}", [P, S], U32, tag="tab_s" if a == 0 else None) for a in range(K_PASSES)]
        list_halves = [slice(0, S // 2), slice(S // 2, S)]
        half_banks = [banks[PACK], banks[0]]
        for a in range(K_PASSES):
            for part in list_halves if a == K_PASSES - 1 else [slice(0, S)]:
                nc.vector.tensor_copy(v_w[a][:, part], tab_w[a][:].bitcast(U32).indirect(entries(list1, part)))
            for part, bank in zip(list_halves, half_banks):
                first_product(0, a, 0, bank, part)
            for t in range(1, PACK):
                first_product(0, a, t, banks[PACK + t])
        for part, bank in zip(list_halves, half_banks):
            scatter(0, 0, bank, part)
        for t in range(1, PACK):
            scatter(0, t, banks[PACK + t])

        for a in range(K_PASSES):
            late = tile(f"late{a}", [P, CHUNK], BF16, tag=f"factor0{a}")
            round_w1(nc.scalar.copy, 1, a, late)
            quantize(w1_w[1][a][:], w1_s[1][a][:], late[:])
            for t in range(PACK):
                first_product(1, a, t, banks[t])

        def gather(b, t, dst, part):
            nc.vector.tensor_copy(dst[:, t, :], page[b][t][:].indirect(entries(list3, part)))

        def add_bias(b, t, dst, src):
            nc.scalar.activation(out=dst[:, t, :], in_=src[:, t, :], func=ACT.Identity, bias=bx_c[:, b, t : t + 1])

        def by_slice(ap):
            return ap.rearrange("p (t m) -> p t m", t=PACK)

        def join(b, t, move=nc.sync.dma_start):
            move(out=joined[b][:, t * T2 : (t + 1) * T2], in_=page[b][t][:])

        def store_page(b, t):
            nc.sync.dma_start(out=page_out[b, t], in_=page[b][t][:])

        def round_page(b, c0, c1):
            interleave(nc.scalar.copy, page_bf[b][:, c0 * PACK : c1 * PACK], by_slice(joined[b])[:, :, c0:c1])

        def quantize_page(b, side):
            w = T2 // 2
            cols = slice(side * w, (side + 1) * w)
            quantize(plane_w[b][:, cols], plane_s[b][:, cols], page_bf[b][:, side * w * PACK : (side + 1) * w * PACK])

        def store_planes(b):
            nc.sync.dma_start(out=out_2[b].rearrange("p m i -> p (m i)").bitcast(I32), in_=plane_w[b][:].bitcast(I32))
            for q in range(QUADS):
                nc.sync.dma_start(
                    out=out_3[b, block_rows(q), :].bitcast(I32),
                    in_=plane_s[b][QUAD * q : QUAD * q + SCALE_ROWS, :].bitcast(I32),
                )

        def second_product(weight, n, b, half, dst, start, stop):
            cols = slice(n * P, (n + 1) * P)
            if weight == W2:
                wide = slice(b * N + n * P, b * N + (n + 1) * P)
                words, scales = w2_w[:, wide].bitcast(FP8X4), w2_s[:, wide]
            elif weight == W3:
                words, scales = w3_w[:, b, 2 * n * P : 2 * (n + 1) * P].bitcast(FP4X4), w3_s[:, b, cols]
            else:
                words, scales = w4_w[:, b, cols].bitcast(FP8X4), w4_s[:, b, cols]
            width = P if weight == W3 else HALF
            for c0 in range(0, HALF, width):
                m_cols = slice(half * HALF + c0, half * HALF + c0 + width)
                nc.tensor.matmul_mx(
                    out=dst[:, c0 : c0 + width], lhsT=words, lhsT_scale=scales,
                    rhs=x_w[b][:, m_cols].bitcast(FP8X4), rhs_scale=x_s[b][:, m_cols],
                    start=(start and c0 == 0), stop=(stop and c0 + width == HALF),
                )

        bank_sums = [((W2, 0), (W2, 1)), ((W3, 0), (W3, 1)), ((W4, 0), (W4, 1)), ((W2, 2), (W3, 2))]
        per_half = len(bank_sums)

        def paired_products(b, half):
            for i, pair in enumerate(bank_sums):
                for side, (weight, n) in enumerate(pair):
                    dst = banks[per_half * half + i][:, side * HALF : (side + 1) * HALF]
                    second_product(weight, n, b, half, dst, b == 0 and side == 0, b == GROUPS - 1 and side == 1)

        last = PACK - 1
        for t in range(PACK):
            join(0, t)
        for t in range(last):
            store_page(0, t)
        for t in range(PACK):
            gather(0, t, by_slice(picked0), slice(0, M))
        for t in range(PACK):
            scatter(1, t, banks[t])
        for t in range(last):
            join(1, t)
        store_page(0, last)
        for t in range(PACK):
            store_page(1, t)

        for b in range(GROUPS):
            interleave(nc.scalar.copy, w2_bf[:, b * N * PACK : (b + 1) * N * PACK], w2_raw[b][:])
        for c0, c1 in ((0, W2_SPLIT), (W2_SPLIT, GROUPS * N)):
            quantize(w2_w[:, c0:c1], w2_s[:, c0:c1], w2_bf[:, c0 * PACK : c1 * PACK])

        for t in range(PACK):
            add_bias(0, t, by_slice(stage[0][:]), by_slice(picked0))
        for side in range(2):
            round_page(0, side * T2 // 2, (side + 1) * T2 // 2)
            quantize_page(0, side)
        store_planes(0)
        x0_bf = joined[0][:, T2 : 2 * T2].bitcast(BF16)
        interleave(nc.scalar.copy, x0_bf, by_slice(stage[0][:]))

        m_halves = [slice(0, HALF), slice(HALF, M)]
        picked1 = [by_slice(joined[0][:, 2 * T2 : 3 * T2]), by_slice(joined[0][:, T2 : 2 * T2])]
        biased1 = [by_slice(stage[0][:, h * PACK * HALF : (h + 1) * PACK * HALF]) for h in range(2)]
        x1_bf = [stage[1][:, h * PACK * HALF : (h + 1) * PACK * HALF] for h in range(2)]
        for t in range(PACK):
            gather(1, t, picked1[0], m_halves[0])
        quantize(x_w[0][:], x_s[0][:], x0_bf)
        for half in range(2):
            paired_products(0, half)
        for t in range(PACK):
            gather(1, t, picked1[1], m_halves[1])
        join(1, last, move=nc.scalar.copy)
        round_page(1, PAGE_CUTS[0], PAGE_CUTS[1])
        quantize_page(1, 0)

        def finish_x(half, copy):
            for t in range(PACK):
                add_bias(1, t, biased1[half], picked1[half])
            interleave(copy, x1_bf[half], biased1[half])
            quantize(x_w[1][:, m_halves[half]], x_s[1][:, m_halves[half]], x1_bf[half])
            paired_products(1, half)

        finish_x(0, nc.scalar.copy)
        round_page(1, PAGE_CUTS[1], PAGE_CUTS[2])
        finish_x(1, nc.vector.tensor_copy)

        out_rows = out_0.rearrange("(n p) m -> p n m", p=P)

        def combine(half):
            y2_bank, y3_bank, y4_bank, n2_bank = banks[per_half * half : per_half * (half + 1)]
            y2 = wgs_turned[:, half * 2 * BANK : half * 2 * BANK + N_TILES * HALF]
            prod = factor[1][2 * half : 2 * half + 2]
            y = tanh_e[2 * half : 2 * half + 2]
            nc.scalar.copy(out=y2[:, 0:BANK], in_=y2_bank[:])
            for b in range(GROUPS):
                second_product(W4, 2, b, half, y2_bank[:, 0:HALF], b == 0, b == GROUPS - 1)
            nc.scalar.copy(out=y2[:, BANK : BANK + HALF], in_=n2_bank[:, 0:HALF])
            nc.vector.tensor_tensor(prod[0][:], y3_bank[:], y2[:, 0:BANK], ALU.mult)
            nc.vector.tensor_tensor(prod[1][:, 0:HALF], n2_bank[:, HALF:BANK], y2[:, BANK : BANK + HALF], ALU.mult)
            nc.vector.tensor_tensor(y[0][:], y4_bank[:], prod[0][:], ALU.add)
            nc.sync.dma_start(out=out_rows[:, 0:2, m_halves[half]], in_=y[0][:].rearrange("p (n m) -> p n m", n=2))
            nc.vector.tensor_tensor(y[1][:, 0:HALF], y2_bank[:, 0:HALF], prod[1][:, 0:HALF], ALU.add)
            nc.sync.dma_start(out=out_rows[:, 2, m_halves[half]], in_=y[1][:, 0:HALF])

        round_page(1, PAGE_CUTS[2], PAGE_CUTS[3])
        combine(0)
        round_page(1, PAGE_CUTS[3], PAGE_CUTS[4])
        quantize_page(1, 1)
        store_planes(1)
        combine(1)
